import numpy as np, ml_dtypes
CORES = [48,49,50,51,52,53,54,55,72,73,74,75,76,77,78,79]
N = 16
ROOT = 9
def setup_inputs(rng):
    return {"x": rng.standard_normal((N, 128, 8), dtype=np.float32).astype(ml_dtypes.bfloat16)}
def reference(x):
    return {"y": np.broadcast_to(x[ROOT], x.shape)}

@@ -1,0 +1,48 @@
+from concourse.bass import DstId, RemoteDMATransfer
+
+SCRATCH = {
+    "buf": ("dram", [128, 8], "bfloat16"),
+}
+SEMAPHORES = ["loaded", "arr", "sent", "stored"]
+
+ROOT_CORE = 73
+RELAYS = {58: (50, 51), 62: (54, 55), 74: (48, 49), 78: (52, 53)}
+RELAY_MASK = {58: 0x000F, 62: 0x00F0, 74: 0x0F00, 78: 0xF000}
+REST = (72, 75, 76, 77, 79)
+
+
+def rank_program(g, core, T, topo):
+    def xfer(dst, mask):
+        rid, pid, _se = topo.addr(dst)
+        return RemoteDMATransfer(dst_ids=[DstId(rid=rid, pnc=pid)], dma_engine_mask=mask,
+                                 remote_sem=T.sem.arr, src=T.buf[:], dst=T.buf[:])
+
+    def store(src):
+        g.sync.dma_start(T.y[:], src).then_inc(T.sem.stored, 16)
+        g.sync.wait_ge(T.sem.stored, 16)
+
+    if core == ROOT_CORE:
+        g.sync.dma_start(T.buf[:], T.x[:]).then_inc(T.sem.loaded, 16)
+        g.wait_ge(T.sem.loaded, 16)
+        g.remote_dma_fused([xfer(r, RELAY_MASK[r]) for r in (58, 62, 74, 78)], local_sem=T.sem.sent)
+        g.remote_dma_fused([xfer(d, 0x3 << (2 * i)) for i, d in enumerate(REST)], local_sem=T.sem.sent)
+        g.wait_ge(T.sem.sent, 26)
+        g.sync.wait_ge(T.sem.sent, 26)
+        store(T.x[:])
+        return
+
+    if core in RELAYS:
+        a, b = RELAYS[core]
+        g.wait_ge(T.sem.arr, 4)
+        g.remote_dma_fused([xfer(a, 0x0F), xfer(b, 0xF0)], local_sem=T.sem.sent)
+        g.wait_ge(T.sem.sent, 8)
+        if T.rank_of(core) is not None:
+            g.sync.wait_ge(T.sem.arr, 4)
+            g.sync.wait_ge(T.sem.sent, 8)
+            store(T.buf[:])
+        return
+
+    if T.rank_of(core) is None:
+        return
+    g.sync.wait_ge(T.sem.arr, 2 if core in REST else 4)
+    store(T.buf[:])

@@ -7,15 +7,15 @@ SEMAPHORES = ["loaded", "arr", "sent", "stored"]
 
 ROOT_CORE = 73
 RELAYS = {58: (50, 51), 62: (54, 55), 74: (48, 49), 78: (52, 53)}
-RELAY_MASK = {58: 0x000F, 62: 0x00F0, 74: 0x0F00, 78: 0xF000}
 REST = (72, 75, 76, 77, 79)
 
 
 def rank_program(g, core, T, topo):
-    def xfer(dst, mask):
-        rid, pid, _se = topo.addr(dst)
-        return RemoteDMATransfer(dst_ids=[DstId(rid=rid, pnc=pid)], dma_engine_mask=mask,
-                                 remote_sem=T.sem.arr, src=T.buf[:], dst=T.buf[:])
+    def send(dsts, mask):
+        ids = [DstId(rid=topo.addr(d)[0], pnc=topo.addr(d)[1]) for d in dsts]
+        g.remote_dma_fused([RemoteDMATransfer(dst_ids=ids, dma_engine_mask=mask, remote_sem=T.sem.arr,
+                                              srcs=[T.buf[:]], dsts=[T.buf[:] for d in dsts])],
+                           local_sem=T.sem.sent)
 
     def store(src):
         g.sync.dma_start(T.y[:], src).then_inc(T.sem.stored, 16)
@@ -24,25 +24,24 @@ def rank_program(g, core, T, topo):
     if core == ROOT_CORE:
         g.sync.dma_start(T.buf[:], T.x[:]).then_inc(T.sem.loaded, 16)
         g.wait_ge(T.sem.loaded, 16)
-        g.remote_dma_fused([xfer(r, RELAY_MASK[r]) for r in (58, 62, 74, 78)], local_sem=T.sem.sent)
-        g.remote_dma_fused([xfer(d, 0x3 << (2 * i)) for i, d in enumerate(REST)], local_sem=T.sem.sent)
-        g.wait_ge(T.sem.sent, 26)
-        g.sync.wait_ge(T.sem.sent, 26)
+        send((58, 62, 74, 78), 0x00FF)
+        send(REST, 0xFF00)
+        g.wait_ge(T.sem.sent, 16)
+        g.sync.wait_ge(T.sem.sent, 16)
         store(T.x[:])
         return
 
     if core in RELAYS:
-        a, b = RELAYS[core]
-        g.wait_ge(T.sem.arr, 4)
-        g.remote_dma_fused([xfer(a, 0x0F), xfer(b, 0xF0)], local_sem=T.sem.sent)
+        g.wait_ge(T.sem.arr, 8)
+        send(RELAYS[core], 0x00FF)
         g.wait_ge(T.sem.sent, 8)
         if T.rank_of(core) is not None:
-            g.sync.wait_ge(T.sem.arr, 4)
+            g.sync.wait_ge(T.sem.arr, 8)
             g.sync.wait_ge(T.sem.sent, 8)
             store(T.buf[:])
         return
 
     if T.rank_of(core) is None:
         return
-    g.sync.wait_ge(T.sem.arr, 2 if core in REST else 4)
+    g.sync.wait_ge(T.sem.arr, 8)
     store(T.buf[:])

from concourse.bass import DstId, RemoteDMATransfer

SCRATCH = {
    "buf": ("dram", [128, 8], "bfloat16"),
}
SEMAPHORES = ["loaded", "arr", "sent", "stored"]

ROOT_CORE = 73
RELAYS = {58: (50, 51), 62: (54, 55), 74: (48, 49), 78: (52, 53)}
REST = (72, 75, 76, 77, 79)


def rank_program(g, core, T, topo):
    def send(dsts, mask):
        ids = [DstId(rid=topo.addr(d)[0], pnc=topo.addr(d)[1]) for d in dsts]
        g.remote_dma_fused([RemoteDMATransfer(dst_ids=ids, dma_engine_mask=mask, remote_sem=T.sem.arr,
                                              srcs=[T.buf[:]], dsts=[T.buf[:] for d in dsts])],
                           local_sem=T.sem.sent)

    def store(src):
        g.sync.dma_start(T.y[:], src).then_inc(T.sem.stored, 16)
        g.sync.wait_ge(T.sem.stored, 16)

    if core == ROOT_CORE:
        g.sync.dma_start(T.buf[:], T.x[:]).then_inc(T.sem.loaded, 16)
        g.wait_ge(T.sem.loaded, 16)
        send((58, 62, 74, 78), 0x00FF)
        send(REST, 0xFF00)
        g.wait_ge(T.sem.sent, 16)
        g.sync.wait_ge(T.sem.sent, 16)
        store(T.x[:])
        return

    if core in RELAYS:
        g.wait_ge(T.sem.arr, 8)
        send(RELAYS[core], 0x00FF)
        g.wait_ge(T.sem.sent, 8)
        if T.rank_of(core) is not None:
            g.sync.wait_ge(T.sem.arr, 8)
            g.sync.wait_ge(T.sem.sent, 8)
            store(T.buf[:])
        return

    if T.rank_of(core) is None:
        return
    g.sync.wait_ge(T.sem.arr, 8)
    store(T.buf[:])
